import numpy as np
import ml_dtypes


def mxq(x, axis, fmt="e4m3"):
    dtype, down = {"e4m3": (ml_dtypes.float8_e4m3fn, 7), "e5m2": (ml_dtypes.float8_e5m2, 14)}[fmt]
    v = np.moveaxis(np.asarray(x, np.float32).astype(ml_dtypes.bfloat16).astype(np.float64), axis, -1)
    blocks = v.reshape(v.shape[:-1] + (-1, 32))
    amax = np.abs(blocks).max(-1, keepdims=True)
    byte = np.maximum(np.where(amax > 0, np.frexp(amax)[1] - 1 + 127, 0) - down, 1)
    scale = np.exp2(byte - 127.0)
    codes = (blocks / scale).astype(np.float32).astype(dtype).astype(np.float64)
    return np.moveaxis((codes * scale).reshape(v.shape), -1, axis)


WIDE = False


def mx_kscale(k):
    if not WIDE:
        return np.ones(k)
    levels = np.array([10, -10, 5, -5, 0])
    if k % 512:
        return np.exp2(np.random.permutation(np.resize(levels, k // 32))).repeat(32)
    a = np.empty((k // 512, 16))
    for p in range(k // 512):
        a[p, :8] = np.random.permutation(np.resize(levels, 8))
        for g in range(8):
            far = levels[np.abs(levels - a[p, g]) >= 10]
            a[p, g + 8] = far[np.random.randint(len(far))]
    return np.exp2(a.ravel()).repeat(32)


def f64(x):
    return np.asarray(x).astype(np.float64)


def striped(idx):
    return np.tile(idx.reshape(-1, 16).T, (8, 1)).astype(np.uint16)


def unstriped(offs):
    return offs[:16].T.reshape(-1).astype(np.int64)


def striped8(idx):
    return np.concatenate([x.reshape(-1, 16).T for x in idx]).astype(np.uint16)


def runs(offs, k):
    lists = np.stack([offs[16 * r : 16 * r + 16].T.reshape(-1) for r in range(8)]).astype(np.int64)
    return lists[np.arange(k) % 512 // 64]


def pack_weight(w):
    k, n = w.shape
    w = f64(np.asarray(w, np.float32).astype(ml_dtypes.bfloat16)).reshape(k // 32, 32, n)
    amax = np.abs(w).max(1)
    byte = np.clip(np.where(amax > 0, np.frexp(amax)[1] - 1 + 127 - 7, 1), 1, 254)
    scaled = (w * np.exp2(127.0 - byte)[:, None, :]).reshape(k, n).astype(np.float32)
    words = np.ascontiguousarray(scaled.reshape(k // 512, 128, 4, n).transpose(0, 1, 3, 2)).astype(ml_dtypes.float8_e4m3fn).view(np.uint8)
    return words, np.ascontiguousarray(byte.astype(np.uint8).reshape(k // 512, 16, n))


def unpack_weight(words, scales):
    g, p, n, _ = words.shape
    vals = np.ascontiguousarray(words).view(ml_dtypes.float8_e4m3fn).astype(np.float64) * np.repeat(np.exp2(scales.astype(np.float64) - 127.0), 8, axis=1)[..., None]
    return vals.transpose(0, 1, 3, 2).reshape(g * 512, n)


def sigmoid(v):
    return 1.0 / (1.0 + np.exp(-np.maximum(v, -700.0)))

def planes(y):
    n, m = y.shape
    v = y.astype(np.float32).astype(ml_dtypes.bfloat16).astype(np.float64).reshape(n // 32, 32, m)
    top = np.abs(v).max(1)
    byte = np.clip(np.where(top > 0, np.frexp(top)[1] - 1 + 127 - 7, 1), 1, 254)
    codes = (v * np.exp2(127.0 - byte)[:, None, :]).reshape(n, m).astype(np.float32).astype(ml_dtypes.float8_e4m3fn).view(np.uint8)
    words = codes.reshape(n // 512, 128, 4, m).transpose(0, 1, 3, 2)
    return np.ascontiguousarray(words), np.ascontiguousarray(byte.astype(np.uint8).reshape(n // 512, 16, m))


K, T, S, N, G, H = 512, 2048, 512, 512, 2048, 512


def setup_inputs():
    n = np.random.standard_normal
    s = mx_kscale(K)[:, None]
    u = mx_kscale(S)
    packed_xT = pack_weight(n((K, T)) * s)
    packed_dT = pack_weight(n((K, G)) / s)
    packed_w1 = pack_weight(n((H, N)) / np.sqrt(2 * H) / u[:, None])
    packed_w2 = pack_weight(n((K, N)) / np.sqrt(2 * K) / s)
    return {
        "x_words": packed_xT[0],
        "x_scales": packed_xT[1],
        "d_words": packed_dT[0],
        "d_scales": packed_dT[1],
        "tau": np.random.uniform(0.3, 0.9, (H, 1)).astype(np.float32),
        "gn": (np.random.uniform(0.5, 1.5, (H, 1)) * u[:, None]).astype(np.float32),
        "w1_words": packed_w1[0],
        "w1_scales": packed_w1[1],
        "w2_words": packed_w2[0],
        "w2_scales": packed_w2[1],
        "sl": np.random.uniform(1.0, 2.0, (N, 1)).astype(np.float32),
        "th": (0.5 * n((N, 1))).astype(np.float32),
        "offs": striped(np.random.permutation(T)[:S]),
        "k1": striped8(np.random.randint(0, G, (8, H))),
        "n1": striped8(np.stack([np.random.permutation(S) for _ in range(8)])),
        "n2": striped8(np.stack([np.random.permutation(S) for _ in range(8)])),
        "two": striped(np.random.permutation(T)[:S]),
        "n3": striped8(np.stack([np.random.permutation(S) for _ in range(8)])),
    }


def reference(x_words, x_scales, d_words, d_scales, tau, gn, w1_words, w1_scales, w2_words, w2_scales, sl, th, offs, k1, n1, n2, two, n3):
    d_k1 = unpack_weight(d_words, d_scales)[np.arange(K)[:, None], runs(k1, K)]
    xq = unpack_weight(x_words, x_scales)[:, unstriped(offs)]
    s = 0.0625 * (d_k1.T @ xq)
    top = s.max(axis=1, keepdims=True)
    ea = np.exp(f64(tau) * (s[np.arange(H)[:, None], runs(n2, H)] - top))
    z = f64(gn) * ((0.5 * (s - (s[np.arange(H)[:, None], runs(n1, H)]))) / (ea + 0.25))
    x_two = unpack_weight(x_words, x_scales)[:, unstriped(two)]
    h = unpack_weight(w1_words, w1_scales).T @ mxq(z, 0, "e4m3") + unpack_weight(w2_words, w2_scales).T @ x_two
    sg = sigmoid(f64(sl) * (h[np.arange(N)[:, None], runs(n3, N)] - f64(th)))
    out_0 = h * sg
    return (out_0,) + planes(out_0)

@@ -1,0 +1,230 @@
+from contextlib import ExitStack
+
+import concourse.mybir as mybir
+
+K, T, S, N, G, H = 512, 2048, 512, 512, 2048, 512
+FLOPS = 2 * K * H * S + 2 * H * N * S + 2 * K * N * S
+
+F32 = mybir.dt.float32
+BF16 = mybir.dt.bfloat16
+I32 = mybir.dt.int32
+U32 = mybir.dt.uint32
+U16 = mybir.dt.uint16
+U8 = mybir.dt.uint8
+FP8X4 = mybir.dt.float8_e4m3fn_x4
+ALU = mybir.AluOpType
+ACT = mybir.ActivationFunctionType
+
+P = 128
+PACK = 4
+HALF = S // 2
+LIST_COLS = S // 16
+CHUNKS = ((0, 256), (256, 384), (384, 512))
+
+
+def tile_picked_kmixeraesa_none_po_kernel(
+    tc, x_words, x_scales, d_words, d_scales, tau, gn, w1_words, w1_scales, w2_words, w2_scales,
+    sl, th, offs, k1, n1, n2, two, n3, out_0, out_1, out_2,
+):
+    nc = tc.nc
+    with ExitStack() as ctx:
+        keep = ctx.enter_context(tc.tile_pool(name="keep", bufs=1))
+        psum = ctx.enter_context(tc.psum_pool(name="psum", bufs=1))
+
+        def sb(name, shape, dtype, tag=None):
+            return keep.tile(shape, dtype, name=name, tag=tag or name, align_bytes=64)
+
+        def words_of(dram):
+            return dram[0].rearrange("p n t -> p (n t)").bitcast(I32)
+
+        def load_list(name, dram):
+            tile = sb(name, [P, LIST_COLS], U16)
+            nc.sync.dma_start(tile[:], dram)
+            return tile
+
+        def load_rows(name, dram):
+            tile = sb(name, [P, PACK], F32)
+            nc.gpsimd.dma_start(tile[:], dram.rearrange("(p t) o -> p (t o)", t=PACK))
+            return tile
+
+        def load_plane(tile, first, dram, queue):
+            rows = dram[0].bitcast(I32)
+            for q in range(4):
+                queue.dma_start(tile[32 * q + first : 32 * q + first + 4, :].bitcast(I32), rows[4 * q : 4 * q + 4, :])
+
+        def dealt(ap):
+            return ap.rearrange("p (m t) -> p t m", t=PACK)
+
+        def by_tile(ap):
+            return ap.rearrange("p (t m) -> p t m", t=PACK)
+
+        def entries(tile, lo, hi):
+            return tile[:, lo // 16 : hi // 16]
+
+        def woven(ap):
+            return ap.rearrange("p (c i t) -> p c t i", i=2, t=PACK)
+
+        def paired(ap):
+            return ap.rearrange("p t (c i) -> p c t i", i=2)
+
+        d_byte_table = sb("d_byte_table", [P, G], U8)
+        x_byte_table = sb("x_byte_table", [P, T], U8)
+        nc.vector.memset(d_byte_table[:].bitcast(I32), 0)
+        nc.vector.memset(x_byte_table[:].bitcast(I32), 0)
+        d_rows = d_scales[0].bitcast(I32)
+        for e in range(2):
+            nc.scalar.dma_start(d_byte_table[e:P:16, :].bitcast(I32), d_rows[e:16:2, :])
+        load_plane(x_byte_table, 0, x_scales, nc.scalar)
+
+        k1_t = load_list("k1_t", k1)
+        offs_t = load_list("offs_t", offs)
+        n2_t = load_list("n2_t", n2)
+        n1_t = load_list("n1_t", n1)
+        n3_t = load_list("n3_t", n3)
+        d_word_table = sb("d_word_table", [P, G], I32)
+        nc.sync.dma_start(d_word_table[:], words_of(d_words))
+        x_word_table = sb("x_word_table", [P, T], I32)
+        nc.sync.dma_start(x_word_table[:], words_of(x_words))
+        two_t = load_list("two_t", two)
+        tau_t = load_rows("tau_t", tau)
+        gn_t = load_rows("gn_t", gn)
+        sl_t = load_rows("sl_t", sl)
+        th_t = load_rows("th_t", th)
+
+        d_bytes = sb("d_bytes", [P, H], U8, tag="bytes")
+        nc.vector.tensor_copy(d_bytes[:], d_byte_table[:].indirect(k1_t[:]))
+        d_plane = sb("d_plane", [P, H], U8)
+        nc.vector.tensor_copy(by_tile(d_plane[:]), dealt(d_bytes[:]))
+        for e in range(2):
+            nc.scalar.dma_start(d_plane[2 + e : P : 32, :].bitcast(I32), d_plane[16 + e : P : 32, :].bitcast(I32))
+        xq_plane = sb("xq_plane", [P, S], U8)
+        nc.vector.tensor_copy(xq_plane[:], x_byte_table[:].indirect(offs_t[:]))
+        d_picked = sb("d_picked", [P, H], U32, tag="picked")
+        nc.vector.tensor_copy(d_picked[:], d_word_table[:].bitcast(U32).indirect(k1_t[:]))
+        d_codes = sb("d_codes", [P, H], U32, tag="codes")
+        nc.vector.tensor_copy(by_tile(d_codes[:]), dealt(d_picked[:]))
+        xq_codes = sb("xq_codes", [P, S], U32)
+        nc.vector.tensor_copy(xq_codes[:], x_word_table[:].bitcast(U32).indirect(offs_t[:]))
+
+        w_raw = sb("w_raw", [P, 2 * N], I32, tag="picked")
+        nc.sync.dma_start(w_raw[:, 0:N], words_of(w2_words))
+        nc.sync.dma_start(w_raw[:, N : 2 * N], words_of(w1_words))
+        w_byte_raw = sb("w_byte_raw", [P, N], U8)
+        nc.gpsimd.memset(w_byte_raw[:].bitcast(I32), 0)
+        load_plane(w_byte_raw, 0, w1_scales, nc.sync)
+        load_plane(w_byte_raw, 4, w2_scales, nc.sync)
+        sbias = sb("sbias", [P, PACK], F32)
+        slth = sb("slth", [P, PACK], F32)
+        nc.gpsimd.tensor_tensor(slth[:], sl_t[:], th_t[:], ALU.mult)
+        nc.gpsimd.tensor_scalar(sbias[:], slth[:], -1.0, 0.0, ALU.mult, ALU.add)
+
+        gain = sb("gain", [P, PACK], F32, tag="bytes")
+        nc.scalar.mul(gain[:], gn_t[:], -0.5)
+        w2_codes = sb("w2_codes", [P, N], U32)
+        w1_codes = sb("w1_codes", [P, N], U32)
+        nc.scalar.copy(by_tile(w2_codes[:]), dealt(w_raw[:, 0:N].bitcast(U32)))
+        nc.scalar.copy(by_tile(w1_codes[:]), dealt(w_raw[:, N : 2 * N].bitcast(U32)))
+
+        s_bank = [psum.tile([P, S], F32, name="s_bank%d" % t, tag="low%d" % t) for t in range(PACK)]
+        for t in range(PACK):
+            cols = slice(t * P, (t + 1) * P)
+            nc.tensor.matmul_mx(
+                out=s_bank[t][:], lhsT=d_codes[:, cols].bitcast(FP8X4), lhsT_scale=d_plane[:, cols],
+                rhs=xq_codes[:].bitcast(FP8X4), rhs_scale=xq_plane[:], start=True, stop=True,
+            )
+
+        x2_plane = sb("x2_plane", [P, S], U8)
+        nc.vector.tensor_copy(x2_plane[:], x_byte_table[:].indirect(two_t[:]))
+
+        s_win = [sb("s_win%d" % t, [P, S], F32) for t in range(PACK)]
+        s_own = [sb("s_own%d" % t, [P, S], F32) for t in range(PACK)]
+        top = [sb("top%d" % t, [P, 1], F32) for t in range(PACK)]
+        ebias = [sb("ebias%d" % t, [P, 1], F32) for t in range(PACK)]
+        ea = sb("ea", [P, PACK, S], F32)
+        diff = sb("diff", [P, PACK, S], F32)
+        num = sb("num", [P, PACK, S], F32)
+        halves = ((0, HALF), (HALF, S))
+        for t in range(PACK):
+            nc.vector.tensor_scalar(s_win[t][:], s_bank[t][:], 0.0625, None, ALU.mult, ALU.max, accum_out=top[t][:])
+            nc.vector.tensor_scalar(ebias[t][:], top[t][:], tau_t[:, t : t + 1], -1.0, ALU.mult, ALU.mult)
+            nc.gpsimd.tensor_scalar(s_own[t][:], s_win[t][:], 1.0, 0.0, ALU.mult, ALU.add)
+            for lo, hi in halves:
+                nc.scalar.activation(
+                    ea[:, t, lo:hi], s_win[t][:].indirect(entries(n2_t, lo, hi)), ACT.Exp,
+                    bias=ebias[t][:], scale=tau_t[:, t : t + 1],
+                )
+
+        x2_codes = sb("x2_codes", [P, S], U32, tag="codes")
+        nc.vector.tensor_copy(x2_codes[:], x_word_table[:].bitcast(U32).indirect(two_t[:]))
+        w_plane = sb("w_plane", [P, N], U8)
+        nc.vector.tensor_copy(by_tile(w_plane[:]), dealt(w_byte_raw[:]))
+        for t in range(PACK):
+            for lo, hi in halves:
+                nc.vector.tensor_tensor(
+                    diff[:, t, lo:hi], s_win[t][:].indirect(entries(n1_t, lo, hi)), s_own[t][:, lo:hi], ALU.subtract
+                )
+        for t in range(PACK):
+            nc.vector.tensor_scalar(num[:, t, :], diff[:, t, :], gain[:, t : t + 1], None, ALU.mult)
+
+        h_bank = [
+            [psum.tile([P, HALF], F32, name="h_bank%d_%d" % (u, t), tag=("low%d", "high%d")[u] % t) for t in range(PACK)]
+            for u in range(2)
+        ]
+        for u, (lo, hi) in enumerate(halves):
+            for t in range(PACK):
+                cols = slice(t * P, (t + 1) * P)
+                nc.tensor.matmul_mx(
+                    out=h_bank[u][t][:], lhsT=w2_codes[:, cols].bitcast(FP8X4), lhsT_scale=w_plane[4:P, cols],
+                    rhs=x2_codes[:, lo:hi].bitcast(FP8X4), rhs_scale=x2_plane[:, lo:hi], start=True, stop=False,
+                )
+
+        for lo, hi in CHUNKS:
+            width = hi - lo
+            u = lo // HALF
+            den2 = sb("den2_%d" % lo, [P, PACK, width], F32)
+            nc.scalar.activation(den2[:], ea[:, :, lo:hi], ACT.Square, bias=0.25)
+            rec = sb("rec%d" % lo, [P, PACK, width], F32)
+            nc.scalar.activation(rec[:], den2[:], ACT.Abs_reciprocal_sqrt)
+            z_woven = sb("z_woven%d" % lo, [P, width * PACK], BF16)
+            nc.vector.tensor_tensor(woven(z_woven[:]), paired(num[:, :, lo:hi]), paired(rec[:]), ALU.mult)
+            z_codes = sb("z_codes%d" % lo, [P, width], U32)
+            z_plane = sb("z_plane%d" % lo, [P, width], U8)
+            nc.vector.quantize_mx(out=z_codes[:].bitcast(FP8X4), scales=z_plane[:], in_=z_woven[:])
+            for t in range(PACK):
+                cols = slice(t * P, (t + 1) * P)
+                nc.tensor.matmul_mx(
+                    out=h_bank[u][t][:, lo - u * HALF : hi - u * HALF],
+                    lhsT=w1_codes[:, cols].bitcast(FP8X4), lhsT_scale=w_plane[:, cols],
+                    rhs=z_codes[:].bitcast(FP8X4), rhs_scale=z_plane[:], start=False, stop=(hi % HALF == 0),
+                )
+
+        h_win = [sb("h_win%d" % t, [P, S], F32) for t in range(PACK)]
+        for u, (lo, hi) in enumerate(halves):
+            for t in range(PACK):
+                nc.vector.tensor_copy(h_win[t][:, lo:hi], h_bank[u][t][:])
+        o_codes = sb("o_codes", [P, S], U32)
+        o_plane = sb("o_plane", [P, S], U8)
+        out_rows = out_0.rearrange("(p t) j -> p t j", t=PACK)
+        out_words = words_of(out_1)
+        for lo, hi in CHUNKS:
+            width = hi - lo
+            u = lo // HALF
+            gate = sb("gate%d" % lo, [P, PACK, width], F32)
+            res = sb("res%d" % lo, [P, PACK, width], F32)
+            for t in range(PACK):
+                nc.scalar.activation(
+                    gate[:, t, :], h_win[t][:].indirect(entries(n3_t, lo, hi)), ACT.Sigmoid,
+                    bias=sbias[:, t : t + 1], scale=sl_t[:, t : t + 1],
+                )
+                nc.vector.tensor_tensor(
+                    res[:, t, :], h_bank[u][t][:, lo - u * HALF : hi - u * HALF], gate[:, t, :], ALU.mult
+                )
+            nc.sync.dma_start(out_rows[:, :, lo:hi], res[:])
+            o_woven = sb("o_woven%d" % lo, [P, width * PACK], BF16)
+            nc.vector.tensor_copy(woven(o_woven[:]), paired(res[:]))
+            nc.vector.quantize_mx(out=o_codes[:, lo:hi].bitcast(FP8X4), scales=o_plane[:, lo:hi], in_=o_woven[:])
+            nc.sync.dma_start(out_words[:, lo:hi], o_codes[:, lo:hi].bitcast(I32))
+        out_bytes = out_2[0].bitcast(I32)
+        for q in range(4):
+            queue = nc.scalar if q % 2 else nc.sync
+            queue.dma_start(out_bytes[4 * q : 4 * q + 4, :], o_plane[32 * q : 32 * q + 4, :].bitcast(I32))

@@ -17,6 +17,7 @@ ACT = mybir.ActivationFunctionType
 
 P = 128
 PACK = 4
+LAST = PACK - 1
 HALF = S // 2
 LIST_COLS = S // 16
 CHUNKS = ((0, 256), (256, 384), (384, 512))
@@ -71,20 +72,18 @@ def tile_picked_kmixeraesa_none_po_kernel(
         x_byte_table = sb("x_byte_table", [P, T], U8)
         nc.vector.memset(d_byte_table[:].bitcast(I32), 0)
         nc.vector.memset(x_byte_table[:].bitcast(I32), 0)
-        d_rows = d_scales[0].bitcast(I32)
-        for e in range(2):
-            nc.scalar.dma_start(d_byte_table[e:P:16, :].bitcast(I32), d_rows[e:16:2, :])
         load_plane(x_byte_table, 0, x_scales, nc.scalar)
 
         k1_t = load_list("k1_t", k1)
+        nc.sync.dma_start(d_byte_table[0:P:8, :].bitcast(I32), d_scales[0].bitcast(I32))
         offs_t = load_list("offs_t", offs)
         n2_t = load_list("n2_t", n2)
-        n1_t = load_list("n1_t", n1)
-        n3_t = load_list("n3_t", n3)
-        d_word_table = sb("d_word_table", [P, G], I32)
+        d_word_table = sb("d_word_table", [P, G], I32, tag="dictionary")
         nc.sync.dma_start(d_word_table[:], words_of(d_words))
+        n1_t = load_list("n1_t", n1)
         x_word_table = sb("x_word_table", [P, T], I32)
         nc.sync.dma_start(x_word_table[:], words_of(x_words))
+        n3_t = load_list("n3_t", n3)
         two_t = load_list("two_t", two)
         tau_t = load_rows("tau_t", tau)
         gn_t = load_rows("gn_t", gn)
@@ -93,16 +92,16 @@ def tile_picked_kmixeraesa_none_po_kernel(
 
         d_bytes = sb("d_bytes", [P, H], U8, tag="bytes")
         nc.vector.tensor_copy(d_bytes[:], d_byte_table[:].indirect(k1_t[:]))
-        d_plane = sb("d_plane", [P, H], U8)
+        d_plane = sb("d_plane", [P, H], U8, tag="plane")
         nc.vector.tensor_copy(by_tile(d_plane[:]), dealt(d_bytes[:]))
-        for e in range(2):
-            nc.scalar.dma_start(d_plane[2 + e : P : 32, :].bitcast(I32), d_plane[16 + e : P : 32, :].bitcast(I32))
-        xq_plane = sb("xq_plane", [P, S], U8)
-        nc.vector.tensor_copy(xq_plane[:], x_byte_table[:].indirect(offs_t[:]))
+        for j in range(1, 4):
+            nc.scalar.dma_start(d_plane[j:P:32, :].bitcast(I32), d_plane[8 * j : P : 32, :].bitcast(I32))
         d_picked = sb("d_picked", [P, H], U32, tag="picked")
         nc.vector.tensor_copy(d_picked[:], d_word_table[:].bitcast(U32).indirect(k1_t[:]))
         d_codes = sb("d_codes", [P, H], U32, tag="codes")
         nc.vector.tensor_copy(by_tile(d_codes[:]), dealt(d_picked[:]))
+        xq_plane = sb("xq_plane", [P, S], U8, tag="dictionary")
+        nc.vector.tensor_copy(xq_plane[:], x_byte_table[:].indirect(offs_t[:]))
         xq_codes = sb("xq_codes", [P, S], U32)
         nc.vector.tensor_copy(xq_codes[:], x_word_table[:].bitcast(U32).indirect(offs_t[:]))
 
@@ -147,24 +146,31 @@ def tile_picked_kmixeraesa_none_po_kernel(
         for t in range(PACK):
             nc.vector.tensor_scalar(s_win[t][:], s_bank[t][:], 0.0625, None, ALU.mult, ALU.max, accum_out=top[t][:])
             nc.vector.tensor_scalar(ebias[t][:], top[t][:], tau_t[:, t : t + 1], -1.0, ALU.mult, ALU.mult)
-            nc.gpsimd.tensor_scalar(s_own[t][:], s_win[t][:], 1.0, 0.0, ALU.mult, ALU.add)
+            factor = gain[:, t : t + 1] if t == LAST else 1.0
+            nc.gpsimd.tensor_scalar(s_own[t][:], s_win[t][:], factor, 0.0, ALU.mult, ALU.add)
             for lo, hi in halves:
                 nc.scalar.activation(
                     ea[:, t, lo:hi], s_win[t][:].indirect(entries(n2_t, lo, hi)), ACT.Exp,
                     bias=ebias[t][:], scale=tau_t[:, t : t + 1],
                 )
 
+        for lo, hi in halves:
+            nc.scalar.activation(diff[:, LAST, lo:hi], s_win[LAST][:].indirect(entries(n1_t, lo, hi)), ACT.Copy)
+
         x2_codes = sb("x2_codes", [P, S], U32, tag="codes")
         nc.vector.tensor_copy(x2_codes[:], x_word_table[:].bitcast(U32).indirect(two_t[:]))
-        w_plane = sb("w_plane", [P, N], U8)
-        nc.vector.tensor_copy(by_tile(w_plane[:]), dealt(w_byte_raw[:]))
-        for t in range(PACK):
+        w_plane = sb("w_plane", [P, N], U8, tag="plane")
+        nc.gpsimd.tensor_copy(by_tile(w_plane[:]), dealt(w_byte_raw[:]))
+        for t in range(LAST):
             for lo, hi in halves:
                 nc.vector.tensor_tensor(
                     diff[:, t, lo:hi], s_win[t][:].indirect(entries(n1_t, lo, hi)), s_own[t][:, lo:hi], ALU.subtract
                 )
-        for t in range(PACK):
+        for t in range(LAST):
             nc.vector.tensor_scalar(num[:, t, :], diff[:, t, :], gain[:, t : t + 1], None, ALU.mult)
+        nc.vector.scalar_tensor_tensor(
+            num[:, LAST, :], diff[:, LAST, :], gain[:, LAST : LAST + 1], s_own[LAST][:], ALU.mult, ALU.subtract
+        )
 
         h_bank = [
             [psum.tile([P, HALF], F32, name="h_bank%d_%d" % (u, t), tag=("low%d", "high%d")[u] % t) for t in range(PACK)]

@@ -17,7 +17,6 @@ ACT = mybir.ActivationFunctionType
 
 P = 128
 PACK = 4
-LAST = PACK - 1
 HALF = S // 2
 LIST_COLS = S // 16
 CHUNKS = ((0, 256), (256, 384), (384, 512))
@@ -83,8 +82,12 @@ def tile_picked_kmixeraesa_none_po_kernel(
         n1_t = load_list("n1_t", n1)
         x_word_table = sb("x_word_table", [P, T], I32)
         nc.sync.dma_start(x_word_table[:], words_of(x_words))
-        n3_t = load_list("n3_t", n3)
         two_t = load_list("two_t", two)
+        w2_raw = sb("w2_raw", [P, N], I32)
+        nc.sync.dma_start(w2_raw[:], words_of(w2_words))
+        w1_raw = sb("w1_raw", [P, N], I32)
+        nc.sync.dma_start(w1_raw[:], words_of(w1_words))
+        n3_t = load_list("n3_t", n3)
         tau_t = load_rows("tau_t", tau)
         gn_t = load_rows("gn_t", gn)
         sl_t = load_rows("sl_t", sl)
@@ -96,18 +99,17 @@ def tile_picked_kmixeraesa_none_po_kernel(
         nc.vector.tensor_copy(by_tile(d_plane[:]), dealt(d_bytes[:]))
         for j in range(1, 4):
             nc.scalar.dma_start(d_plane[j:P:32, :].bitcast(I32), d_plane[8 * j : P : 32, :].bitcast(I32))
-        d_picked = sb("d_picked", [P, H], U32, tag="picked")
+        d_picked = sb("d_picked", [P, H], U32)
         nc.vector.tensor_copy(d_picked[:], d_word_table[:].bitcast(U32).indirect(k1_t[:]))
         d_codes = sb("d_codes", [P, H], U32, tag="codes")
         nc.vector.tensor_copy(by_tile(d_codes[:]), dealt(d_picked[:]))
         xq_plane = sb("xq_plane", [P, S], U8, tag="dictionary")
         nc.vector.tensor_copy(xq_plane[:], x_byte_table[:].indirect(offs_t[:]))
         xq_codes = sb("xq_codes", [P, S], U32)
-        nc.vector.tensor_copy(xq_codes[:], x_word_table[:].bitcast(U32).indirect(offs_t[:]))
+        halves = ((0, HALF), (HALF, S))
+        for lo, hi in halves:
+            nc.vector.tensor_copy(xq_codes[:, lo:hi], x_word_table[:].bitcast(U32).indirect(entries(offs_t, lo, hi)))
 
-        w_raw = sb("w_raw", [P, 2 * N], I32, tag="picked")
-        nc.sync.dma_start(w_raw[:, 0:N], words_of(w2_words))
-        nc.sync.dma_start(w_raw[:, N : 2 * N], words_of(w1_words))
         w_byte_raw = sb("w_byte_raw", [P, N], U8)
         nc.gpsimd.memset(w_byte_raw[:].bitcast(I32), 0)
         load_plane(w_byte_raw, 0, w1_scales, nc.sync)
@@ -121,16 +123,17 @@ def tile_picked_kmixeraesa_none_po_kernel(
         nc.scalar.mul(gain[:], gn_t[:], -0.5)
         w2_codes = sb("w2_codes", [P, N], U32)
         w1_codes = sb("w1_codes", [P, N], U32)
-        nc.scalar.copy(by_tile(w2_codes[:]), dealt(w_raw[:, 0:N].bitcast(U32)))
-        nc.scalar.copy(by_tile(w1_codes[:]), dealt(w_raw[:, N : 2 * N].bitcast(U32)))
+        nc.scalar.copy(by_tile(w2_codes[:]), dealt(w2_raw[:].bitcast(U32)))
+        nc.scalar.copy(by_tile(w1_codes[:]), dealt(w1_raw[:].bitcast(U32)))
 
         s_bank = [psum.tile([P, S], F32, name="s_bank%d" % t, tag="low%d" % t) for t in range(PACK)]
         for t in range(PACK):
             cols = slice(t * P, (t + 1) * P)
-            nc.tensor.matmul_mx(
-                out=s_bank[t][:], lhsT=d_codes[:, cols].bitcast(FP8X4), lhsT_scale=d_plane[:, cols],
-                rhs=xq_codes[:].bitcast(FP8X4), rhs_scale=xq_plane[:], start=True, stop=True,
-            )
+            for lo, hi in halves:
+                nc.tensor.matmul_mx(
+                    out=s_bank[t][:, lo:hi], lhsT=d_codes[:, cols].bitcast(FP8X4), lhsT_scale=d_plane[:, cols],
+                    rhs=xq_codes[:, lo:hi].bitcast(FP8X4), rhs_scale=xq_plane[:, lo:hi], start=True, stop=True,
+                )
 
         x2_plane = sb("x2_plane", [P, S], U8)
         nc.vector.tensor_copy(x2_plane[:], x_byte_table[:].indirect(two_t[:]))
@@ -142,35 +145,27 @@ def tile_picked_kmixeraesa_none_po_kernel(
         ea = sb("ea", [P, PACK, S], F32)
         diff = sb("diff", [P, PACK, S], F32)
         num = sb("num", [P, PACK, S], F32)
-        halves = ((0, HALF), (HALF, S))
         for t in range(PACK):
             nc.vector.tensor_scalar(s_win[t][:], s_bank[t][:], 0.0625, None, ALU.mult, ALU.max, accum_out=top[t][:])
             nc.vector.tensor_scalar(ebias[t][:], top[t][:], tau_t[:, t : t + 1], -1.0, ALU.mult, ALU.mult)
-            factor = gain[:, t : t + 1] if t == LAST else 1.0
-            nc.gpsimd.tensor_scalar(s_own[t][:], s_win[t][:], factor, 0.0, ALU.mult, ALU.add)
+            nc.gpsimd.tensor_scalar(s_own[t][:], s_win[t][:], 1.0, 0.0, ALU.mult, ALU.add)
             for lo, hi in halves:
                 nc.scalar.activation(
                     ea[:, t, lo:hi], s_win[t][:].indirect(entries(n2_t, lo, hi)), ACT.Exp,
                     bias=ebias[t][:], scale=tau_t[:, t : t + 1],
                 )
 
-        for lo, hi in halves:
-            nc.scalar.activation(diff[:, LAST, lo:hi], s_win[LAST][:].indirect(entries(n1_t, lo, hi)), ACT.Copy)
-
         x2_codes = sb("x2_codes", [P, S], U32, tag="codes")
         nc.vector.tensor_copy(x2_codes[:], x_word_table[:].bitcast(U32).indirect(two_t[:]))
         w_plane = sb("w_plane", [P, N], U8, tag="plane")
         nc.gpsimd.tensor_copy(by_tile(w_plane[:]), dealt(w_byte_raw[:]))
-        for t in range(LAST):
+        for t in range(PACK):
             for lo, hi in halves:
                 nc.vector.tensor_tensor(
                     diff[:, t, lo:hi], s_win[t][:].indirect(entries(n1_t, lo, hi)), s_own[t][:, lo:hi], ALU.subtract
                 )
-        for t in range(LAST):
+        for t in range(PACK):
             nc.vector.tensor_scalar(num[:, t, :], diff[:, t, :], gain[:, t : t + 1], None, ALU.mult)
-        nc.vector.scalar_tensor_tensor(
-            num[:, LAST, :], diff[:, LAST, :], gain[:, LAST : LAST + 1], s_own[LAST][:], ALU.mult, ALU.subtract
-        )
 
         h_bank = [
             [psum.tile([P, HALF], F32, name="h_bank%d_%d" % (u, t), tag=("low%d", "high%d")[u] % t) for t in range(PACK)]

from contextlib import ExitStack

import concourse.mybir as mybir

K, T, S, N, G, H = 512, 2048, 512, 512, 2048, 512
FLOPS = 2 * K * H * S + 2 * H * N * S + 2 * K * N * S

F32 = mybir.dt.float32
BF16 = mybir.dt.bfloat16
I32 = mybir.dt.int32
U32 = mybir.dt.uint32
U16 = mybir.dt.uint16
U8 = mybir.dt.uint8
FP8X4 = mybir.dt.float8_e4m3fn_x4
ALU = mybir.AluOpType
ACT = mybir.ActivationFunctionType

P = 128
PACK = 4
HALF = S // 2
LIST_COLS = S // 16
CHUNKS = ((0, 256), (256, 384), (384, 512))


def tile_picked_kmixeraesa_none_po_kernel(
    tc, x_words, x_scales, d_words, d_scales, tau, gn, w1_words, w1_scales, w2_words, w2_scales,
    sl, th, offs, k1, n1, n2, two, n3, out_0, out_1, out_2,
):
    nc = tc.nc
    with ExitStack() as ctx:
        keep = ctx.enter_context(tc.tile_pool(name="keep", bufs=1))
        psum = ctx.enter_context(tc.psum_pool(name="psum", bufs=1))

        def sb(name, shape, dtype, tag=None):
            return keep.tile(shape, dtype, name=name, tag=tag or name, align_bytes=64)

        def words_of(dram):
            return dram[0].rearrange("p n t -> p (n t)").bitcast(I32)

        def load_list(name, dram):
            tile = sb(name, [P, LIST_COLS], U16)
            nc.sync.dma_start(tile[:], dram)
            return tile

        def load_rows(name, dram):
            tile = sb(name, [P, PACK], F32)
            nc.gpsimd.dma_start(tile[:], dram.rearrange("(p t) o -> p (t o)", t=PACK))
            return tile

        def load_plane(tile, first, dram, queue):
            rows = dram[0].bitcast(I32)
            for q in range(4):
                queue.dma_start(tile[32 * q + first : 32 * q + first + 4, :].bitcast(I32), rows[4 * q : 4 * q + 4, :])

        def dealt(ap):
            return ap.rearrange("p (m t) -> p t m", t=PACK)

        def by_tile(ap):
            return ap.rearrange("p (t m) -> p t m", t=PACK)

        def entries(tile, lo, hi):
            return tile[:, lo // 16 : hi // 16]

        def woven(ap):
            return ap.rearrange("p (c i t) -> p c t i", i=2, t=PACK)

        def paired(ap):
            return ap.rearrange("p t (c i) -> p c t i", i=2)

        d_byte_table = sb("d_byte_table", [P, G], U8)
        x_byte_table = sb("x_byte_table", [P, T], U8)
        nc.vector.memset(d_byte_table[:].bitcast(I32), 0)
        nc.vector.memset(x_byte_table[:].bitcast(I32), 0)
        load_plane(x_byte_table, 0, x_scales, nc.scalar)

        k1_t = load_list("k1_t", k1)
        nc.sync.dma_start(d_byte_table[0:P:8, :].bitcast(I32), d_scales[0].bitcast(I32))
        offs_t = load_list("offs_t", offs)
        n2_t = load_list("n2_t", n2)
        d_word_table = sb("d_word_table", [P, G], I32, tag="dictionary")
        nc.sync.dma_start(d_word_table[:], words_of(d_words))
        n1_t = load_list("n1_t", n1)
        x_word_table = sb("x_word_table", [P, T], I32)
        nc.sync.dma_start(x_word_table[:], words_of(x_words))
        two_t = load_list("two_t", two)
        w2_raw = sb("w2_raw", [P, N], I32)
        nc.sync.dma_start(w2_raw[:], words_of(w2_words))
        w1_raw = sb("w1_raw", [P, N], I32)
        nc.sync.dma_start(w1_raw[:], words_of(w1_words))
        n3_t = load_list("n3_t", n3)
        tau_t = load_rows("tau_t", tau)
        gn_t = load_rows("gn_t", gn)
        sl_t = load_rows("sl_t", sl)
        th_t = load_rows("th_t", th)

        d_bytes = sb("d_bytes", [P, H], U8, tag="bytes")
        nc.vector.tensor_copy(d_bytes[:], d_byte_table[:].indirect(k1_t[:]))
        d_plane = sb("d_plane", [P, H], U8, tag="plane")
        nc.vector.tensor_copy(by_tile(d_plane[:]), dealt(d_bytes[:]))
        for j in range(1, 4):
            nc.scalar.dma_start(d_plane[j:P:32, :].bitcast(I32), d_plane[8 * j : P : 32, :].bitcast(I32))
        d_picked = sb("d_picked", [P, H], U32)
        nc.vector.tensor_copy(d_picked[:], d_word_table[:].bitcast(U32).indirect(k1_t[:]))
        d_codes = sb("d_codes", [P, H], U32, tag="codes")
        nc.vector.tensor_copy(by_tile(d_codes[:]), dealt(d_picked[:]))
        xq_plane = sb("xq_plane", [P, S], U8, tag="dictionary")
        nc.vector.tensor_copy(xq_plane[:], x_byte_table[:].indirect(offs_t[:]))
        xq_codes = sb("xq_codes", [P, S], U32)
        halves = ((0, HALF), (HALF, S))
        for lo, hi in halves:
            nc.vector.tensor_copy(xq_codes[:, lo:hi], x_word_table[:].bitcast(U32).indirect(entries(offs_t, lo, hi)))

        w_byte_raw = sb("w_byte_raw", [P, N], U8)
        nc.gpsimd.memset(w_byte_raw[:].bitcast(I32), 0)
        load_plane(w_byte_raw, 0, w1_scales, nc.sync)
        load_plane(w_byte_raw, 4, w2_scales, nc.sync)
        sbias = sb("sbias", [P, PACK], F32)
        slth = sb("slth", [P, PACK], F32)
        nc.gpsimd.tensor_tensor(slth[:], sl_t[:], th_t[:], ALU.mult)
        nc.gpsimd.tensor_scalar(sbias[:], slth[:], -1.0, 0.0, ALU.mult, ALU.add)

        gain = sb("gain", [P, PACK], F32, tag="bytes")
        nc.scalar.mul(gain[:], gn_t[:], -0.5)
        w2_codes = sb("w2_codes", [P, N], U32)
        w1_codes = sb("w1_codes", [P, N], U32)
        nc.scalar.copy(by_tile(w2_codes[:]), dealt(w2_raw[:].bitcast(U32)))
        nc.scalar.copy(by_tile(w1_codes[:]), dealt(w1_raw[:].bitcast(U32)))

        s_bank = [psum.tile([P, S], F32, name="s_bank%d" % t, tag="low%d" % t) for t in range(PACK)]
        for t in range(PACK):
            cols = slice(t * P, (t + 1) * P)
            for lo, hi in halves:
                nc.tensor.matmul_mx(
                    out=s_bank[t][:, lo:hi], lhsT=d_codes[:, cols].bitcast(FP8X4), lhsT_scale=d_plane[:, cols],
                    rhs=xq_codes[:, lo:hi].bitcast(FP8X4), rhs_scale=xq_plane[:, lo:hi], start=True, stop=True,
                )

        x2_plane = sb("x2_plane", [P, S], U8)
        nc.vector.tensor_copy(x2_plane[:], x_byte_table[:].indirect(two_t[:]))

        s_win = [sb("s_win%d" % t, [P, S], F32) for t in range(PACK)]
        s_own = [sb("s_own%d" % t, [P, S], F32) for t in range(PACK)]
        top = [sb("top%d" % t, [P, 1], F32) for t in range(PACK)]
        ebias = [sb("ebias%d" % t, [P, 1], F32) for t in range(PACK)]
        ea = sb("ea", [P, PACK, S], F32)
        diff = sb("diff", [P, PACK, S], F32)
        num = sb("num", [P, PACK, S], F32)
        for t in range(PACK):
            nc.vector.tensor_scalar(s_win[t][:], s_bank[t][:], 0.0625, None, ALU.mult, ALU.max, accum_out=top[t][:])
            nc.vector.tensor_scalar(ebias[t][:], top[t][:], tau_t[:, t : t + 1], -1.0, ALU.mult, ALU.mult)
            nc.gpsimd.tensor_scalar(s_own[t][:], s_win[t][:], 1.0, 0.0, ALU.mult, ALU.add)
            for lo, hi in halves:
                nc.scalar.activation(
                    ea[:, t, lo:hi], s_win[t][:].indirect(entries(n2_t, lo, hi)), ACT.Exp,
                    bias=ebias[t][:], scale=tau_t[:, t : t + 1],
                )

        x2_codes = sb("x2_codes", [P, S], U32, tag="codes")
        nc.vector.tensor_copy(x2_codes[:], x_word_table[:].bitcast(U32).indirect(two_t[:]))
        w_plane = sb("w_plane", [P, N], U8, tag="plane")
        nc.gpsimd.tensor_copy(by_tile(w_plane[:]), dealt(w_byte_raw[:]))
        for t in range(PACK):
            for lo, hi in halves:
                nc.vector.tensor_tensor(
                    diff[:, t, lo:hi], s_win[t][:].indirect(entries(n1_t, lo, hi)), s_own[t][:, lo:hi], ALU.subtract
                )
        for t in range(PACK):
            nc.vector.tensor_scalar(num[:, t, :], diff[:, t, :], gain[:, t : t + 1], None, ALU.mult)

        h_bank = [
            [psum.tile([P, HALF], F32, name="h_bank%d_%d" % (u, t), tag=("low%d", "high%d")[u] % t) for t in range(PACK)]
            for u in range(2)
        ]
        for u, (lo, hi) in enumerate(halves):
            for t in range(PACK):
                cols = slice(t * P, (t + 1) * P)
                nc.tensor.matmul_mx(
                    out=h_bank[u][t][:], lhsT=w2_codes[:, cols].bitcast(FP8X4), lhsT_scale=w_plane[4:P, cols],
                    rhs=x2_codes[:, lo:hi].bitcast(FP8X4), rhs_scale=x2_plane[:, lo:hi], start=True, stop=False,
                )

        for lo, hi in CHUNKS:
            width = hi - lo
            u = lo // HALF
            den2 = sb("den2_%d" % lo, [P, PACK, width], F32)
            nc.scalar.activation(den2[:], ea[:, :, lo:hi], ACT.Square, bias=0.25)
            rec = sb("rec%d" % lo, [P, PACK, width], F32)
            nc.scalar.activation(rec[:], den2[:], ACT.Abs_reciprocal_sqrt)
            z_woven = sb("z_woven%d" % lo, [P, width * PACK], BF16)
            nc.vector.tensor_tensor(woven(z_woven[:]), paired(num[:, :, lo:hi]), paired(rec[:]), ALU.mult)
            z_codes = sb("z_codes%d" % lo, [P, width], U32)
            z_plane = sb("z_plane%d" % lo, [P, width], U8)
            nc.vector.quantize_mx(out=z_codes[:].bitcast(FP8X4), scales=z_plane[:], in_=z_woven[:])
            for t in range(PACK):
                cols = slice(t * P, (t + 1) * P)
                nc.tensor.matmul_mx(
                    out=h_bank[u][t][:, lo - u * HALF : hi - u * HALF],
                    lhsT=w1_codes[:, cols].bitcast(FP8X4), lhsT_scale=w_plane[:, cols],
                    rhs=z_codes[:].bitcast(FP8X4), rhs_scale=z_plane[:], start=False, stop=(hi % HALF == 0),
                )

        h_win = [sb("h_win%d" % t, [P, S], F32) for t in range(PACK)]
        for u, (lo, hi) in enumerate(halves):
            for t in range(PACK):
                nc.vector.tensor_copy(h_win[t][:, lo:hi], h_bank[u][t][:])
        o_codes = sb("o_codes", [P, S], U32)
        o_plane = sb("o_plane", [P, S], U8)
        out_rows = out_0.rearrange("(p t) j -> p t j", t=PACK)
        out_words = words_of(out_1)
        for lo, hi in CHUNKS:
            width = hi - lo
            u = lo // HALF
            gate = sb("gate%d" % lo, [P, PACK, width], F32)
            res = sb("res%d" % lo, [P, PACK, width], F32)
            for t in range(PACK):
                nc.scalar.activation(
                    gate[:, t, :], h_win[t][:].indirect(entries(n3_t, lo, hi)), ACT.Sigmoid,
                    bias=sbias[:, t : t + 1], scale=sl_t[:, t : t + 1],
                )
                nc.vector.tensor_tensor(
                    res[:, t, :], h_bank[u][t][:, lo - u * HALF : hi - u * HALF], gate[:, t, :], ALU.mult
                )
            nc.sync.dma_start(out_rows[:, :, lo:hi], res[:])
            o_woven = sb("o_woven%d" % lo, [P, width * PACK], BF16)
            nc.vector.tensor_copy(woven(o_woven[:]), paired(res[:]))
            nc.vector.quantize_mx(out=o_codes[:, lo:hi].bitcast(FP8X4), scales=o_plane[:, lo:hi], in_=o_woven[:])
            nc.sync.dma_start(out_words[:, lo:hi], o_codes[:, lo:hi].bitcast(I32))
        out_bytes = out_2[0].bitcast(I32)
        for q in range(4):
            queue = nc.scalar if q % 2 else nc.sync
            queue.dma_start(out_bytes[4 * q : 4 * q + 4, :], o_plane[32 * q : 32 * q + 4, :].bitcast(I32))
